import numpy as np
import ml_dtypes


def mxq(x, axis, fmt="e4m3"):
    dtype, down = {"e4m3": (ml_dtypes.float8_e4m3fn, 7), "e5m2": (ml_dtypes.float8_e5m2, 14)}[fmt]
    v = np.moveaxis(np.asarray(x, np.float32).astype(ml_dtypes.bfloat16).astype(np.float64), axis, -1)
    blocks = v.reshape(v.shape[:-1] + (-1, 32))
    amax = np.abs(blocks).max(-1, keepdims=True)
    byte = np.maximum(np.where(amax > 0, np.frexp(amax)[1] - 1 + 127, 0) - down, 1)
    scale = np.exp2(byte - 127.0)
    codes = (blocks / scale).astype(np.float32).astype(dtype).astype(np.float64)
    return np.moveaxis((codes * scale).reshape(v.shape), -1, axis)


WIDE = False


def mx_kscale(k):
    if not WIDE:
        return np.ones(k)
    levels = np.array([10, -10, 5, -5, 0])
    if k % 512:
        return np.exp2(np.random.permutation(np.resize(levels, k // 32))).repeat(32)
    a = np.empty((k // 512, 16))
    for p in range(k // 512):
        a[p, :8] = np.random.permutation(np.resize(levels, 8))
        for g in range(8):
            far = levels[np.abs(levels - a[p, g]) >= 10]
            a[p, g + 8] = far[np.random.randint(len(far))]
    return np.exp2(a.ravel()).repeat(32)


def f64(x):
    return np.asarray(x).astype(np.float64)


def striped(idx):
    return np.tile(idx.reshape(-1, 16).T, (8, 1)).astype(np.uint16)


def unstriped(offs):
    return offs[:16].T.reshape(-1).astype(np.int64)


def relu(v):
    return np.maximum(v, 0.0)


K, T, H, N = 512, 256, 512, 256


def setup_inputs():
    n = np.random.standard_normal
    s = mx_kscale(K)[:, None]
    u = mx_kscale(H)
    idx = np.random.permutation(H)
    v = np.empty(H)
    v[idx] = u
    return {
        "xT": (n((K, T)) * s).astype(np.float32),
        "w1": (n((K, H)) / np.sqrt(K) / s * v).astype(np.float32),
        "w2": (n((H, N)) / np.sqrt(H) / u[:, None]).astype(np.float32),
        "offs": striped(idx),
    }


def reference(xT, w1, w2, offs):
    idx = unstriped(offs)
    h = relu(mxq(f64(w1), 0, "e4m3").T @ mxq(f64(xT), 0, "e4m3"))
    return mxq(f64(w2), 0, "e4m3").T @ mxq(h[idx], 0, "e4m3")

@@ -1,0 +1,137 @@
+from contextlib import ExitStack
+
+import concourse.mybir as mybir
+from concourse.masks import make_identity
+
+K, T, H, N = 512, 256, 512, 256
+P = 128
+PACK = 4
+FLOPS = 2 * K * H * T + 2 * H * N * T
+
+F32 = mybir.dt.float32
+BF16 = mybir.dt.bfloat16
+U32 = mybir.dt.uint32
+U16 = mybir.dt.uint16
+U8 = mybir.dt.uint8
+FP8X4 = mybir.dt.float8_e4m3fn_x4
+RELU = mybir.ActivationFunctionType.Relu
+
+X_SPLIT = 128
+W1_SPLIT = 344
+
+
+def tile_picked_shuffle_mlp_relu_perm_l_kernel(tc, xT, w1, w2, offs, out):
+    nc = tc.nc
+    with ExitStack() as ctx:
+        keep = ctx.enter_context(tc.tile_pool(name="keep", bufs=1))
+        psum = ctx.enter_context(tc.psum_pool(name="psum", bufs=1))
+
+        offsets = keep.tile([P, H // 16], U16, name="offsets")
+
+        w1_rows = w1.rearrange("(p j) c -> p j c", j=PACK)
+        w1_raw = []
+        for u in range(2):
+            half = keep.tile([P, 2, H], F32, name=f"w1_raw{u}")
+            nc.sync.dma_start(out=half[:], in_=w1_rows[:, 2 * u : 2 * u + 2, :])
+            w1_raw.append(half)
+        x_rows = xT.rearrange("(p j) t -> p j t", j=PACK)
+        x_raw = []
+        for u in range(2):
+            half = keep.tile([P, 2, T], F32, name=f"x_raw{u}")
+            nc.sync.dma_start(out=half[:], in_=x_rows[:, 2 * u : 2 * u + 2, :])
+            x_raw.append(half)
+        nc.sync.dma_start(offsets[:], offs)
+        w2_raw = keep.tile([P, PACK, N], F32, name="w2_raw")
+        nc.sync.dma_start(out=w2_raw[:], in_=w2.rearrange("(p j) m -> p j m", j=PACK))
+
+        spark = keep.tile([P, 1], F32, name="spark")
+        nc.vector.memset(spark[:], 0.0)
+        spark_out = keep.tile([P, 1], F32, name="spark_out")
+        nc.scalar.activation(spark_out[:], spark[:], RELU)
+        ident = keep.tile([P, P], F32, name="ident")
+        make_identity(nc, ident[:])
+
+        w1_g = keep.tile([P, H, PACK], BF16, name="w1_g", align_bytes=64)
+        w1_codes = keep.tile([P, H], U32, name="w1_codes", align_bytes=64)
+        w1_scales = keep.tile([P, H], U8, name="w1_scales", align_bytes=64)
+        for u in range(2):
+            js = slice(2 * u, 2 * u + 2)
+            nc.vector.tensor_copy(w1_g[:, 0:W1_SPLIT, js], w1_raw[u][:, :, 0:W1_SPLIT].rearrange("p j c -> p c j"))
+            nc.scalar.copy(w1_g[:, W1_SPLIT:H, js], w1_raw[u][:, :, W1_SPLIT:H].rearrange("p j c -> p c j"))
+        nc.vector.quantize_mx(out=w1_codes[:].bitcast(FP8X4), scales=w1_scales[:], in_=w1_g[:].rearrange("p c j -> p (c j)"))
+
+        x_g = keep.tile([P, T, PACK], BF16, name="x_g", align_bytes=64)
+        x_codes = keep.tile([P, T], U32, name="x_codes", align_bytes=64)
+        x_scales = keep.tile([P, T], U8, name="x_scales", align_bytes=64)
+        for u in range(2):
+            js = slice(2 * u, 2 * u + 2)
+            nc.vector.tensor_copy(x_g[:, 0:X_SPLIT, js], x_raw[u][:, :, 0:X_SPLIT].rearrange("p j t -> p t j"))
+            nc.scalar.copy(x_g[:, X_SPLIT:T, js], x_raw[u][:, :, X_SPLIT:T].rearrange("p j t -> p t j"))
+        for e in range(2):
+            ts = slice(e * P, (e + 1) * P)
+            nc.vector.quantize_mx(out=x_codes[:, ts].bitcast(FP8X4), scales=x_scales[:, ts], in_=x_g[:, ts, :].rearrange("p t j -> p (t j)"))
+
+        h_pairs = keep.tile([P, H, 2], BF16, name="h_pairs")
+        for q in range(4):
+            cs = slice(q * P, (q + 1) * P)
+            prod = psum.tile([P, 2, P], F32, name=f"prod{q}")
+            for e in range(2):
+                ts = slice(e * P, (e + 1) * P)
+                nc.tensor.matmul_mx(out=prod[:, e, :], lhsT=x_codes[:, ts].bitcast(FP8X4), lhsT_scale=x_scales[:, ts], rhs=w1_codes[:, cs].bitcast(FP8X4), rhs_scale=w1_scales[:, cs], start=True, stop=True)
+            if q % 2 == 0:
+                nc.scalar.activation(h_pairs[:, cs, :], prod[:].rearrange("p e c -> p c e"), RELU)
+            else:
+                nc.vector.tensor_scalar_max(h_pairs[:, cs, :], prod[:].rearrange("p e c -> p c e"), 0.0)
+
+        w2_g = keep.tile([P, N, PACK], BF16, name="w2_g", align_bytes=64)
+        w2_codes = keep.tile([P, N], U32, name="w2_codes", align_bytes=64)
+        w2_scales = keep.tile([P, N], U8, name="w2_scales", align_bytes=64)
+        nc.scalar.copy(w2_g[:], w2_raw[:].rearrange("p j m -> p m j"))
+
+        picked = keep.tile([P, PACK, P, 2], BF16, name="picked")
+        words = picked[:].rearrange("p t m e -> p t (m e)").bitcast(U32)
+        window = h_pairs[:].rearrange("p c e -> p (c e)").bitcast(U32)
+        for a in range(2):
+            nc.vector.tensor_copy(words[:, :, 64 * a : 64 * a + 64].rearrange("p t m -> p m t"), window.indirect(offsets[:, 16 * a : 16 * a + 16]))
+
+        nc.vector.quantize_mx(out=w2_codes[:].bitcast(FP8X4), scales=w2_scales[:], in_=w2_g[:].rearrange("p m j -> p (m j)"))
+
+        hq_g = keep.tile([P, T, PACK], BF16, name="hq_g", align_bytes=64)
+        h_codes = keep.tile([P, T], U32, name="h_codes", align_bytes=64)
+        h_scales = keep.tile([P, T], U8, name="h_scales", align_bytes=64)
+        picked_words = picked[:].rearrange("p t m e -> p t (m e)").bitcast(F32)
+        turned = []
+        for u in range(2):
+            pair = psum.tile([P, 2, P], F32, name=f"turned{u}")
+            for t in range(2):
+                nc.tensor.transpose(pair[:, t, :], picked_words[:, 2 * u + t, :], ident[:])
+            turned.append(pair[:].bitcast(BF16).rearrange("p t (n e) -> p e n t", e=2))
+        for e in range(2):
+            ts = slice(e * P, (e + 1) * P)
+            nc.vector.tensor_copy(hq_g[:, ts, 0:2], turned[0][:, e, :, :])
+            nc.scalar.copy(hq_g[:, ts, 2:4], turned[1][:, e, :, :])
+        out_rows = out.rearrange("(b m) t -> m b t", b=2)
+        for e in range(2):
+            ts = slice(e * P, (e + 1) * P)
+            nc.vector.quantize_mx(out=h_codes[:, ts].bitcast(FP8X4), scales=h_scales[:, ts], in_=hq_g[:, ts, :].rearrange("p t j -> p (t j)"))
+            results = []
+            for b in range(2):
+                ms = slice(b * P, (b + 1) * P)
+                if e == 0 and b == 1:
+                    res = results[0]
+                elif e == 0:
+                    res = psum.tile([P, 2, P], F32, name="res0")
+                else:
+                    res = psum.tile([P, 2, P], F32, name=f"res1{b}", tag=["res1", "prod0"][b])
+                results.append(res)
+                nc.tensor.matmul_mx(out=res[:, b, :], lhsT=w2_codes[:, ms].bitcast(FP8X4), lhsT_scale=w2_scales[:, ms], rhs=h_codes[:, ts].bitcast(FP8X4), rhs_scale=h_scales[:, ts], start=True, stop=True)
+            if e == 0:
+                o0 = keep.tile([P, 2, P], F32, name="o0")
+                nc.scalar.copy(o0[:], results[0][:])
+                nc.sync.dma_start(out=out_rows[:, :, ts], in_=o0[:])
+            else:
+                o1 = [keep.tile([P, P], F32, name=f"o1{b}") for b in range(2)]
+                nc.scalar.copy(o1[0][:], results[0][:, 0, :])
+                nc.vector.tensor_copy(o1[1][:], results[1][:, 1, :])
+                nc.scalar.dma_start(out=out_rows[:, 0, ts], in_=o1[0][:])
+                nc.sync.dma_start(out=out_rows[:, 1, ts], in_=o1[1][:])

@@ -15,9 +15,7 @@ U16 = mybir.dt.uint16
 U8 = mybir.dt.uint8
 FP8X4 = mybir.dt.float8_e4m3fn_x4
 RELU = mybir.ActivationFunctionType.Relu
-
-X_SPLIT = 128
-W1_SPLIT = 344
+COPY = mybir.ActivationFunctionType.Copy
 
 
 def tile_picked_shuffle_mlp_relu_perm_l_kernel(tc, xT, w1, w2, offs, out):
@@ -31,18 +29,12 @@ def tile_picked_shuffle_mlp_relu_perm_l_kernel(tc, xT, w1, w2, offs, out):
         w1_rows = w1.rearrange("(p j) c -> p j c", j=PACK)
         w1_raw = []
         for u in range(2):
-            half = keep.tile([P, 2, H], F32, name=f"w1_raw{u}")
+            half = keep.tile([P, 2, H], F32, name=f"w1_raw{u}", tag=["early", "late"][u])
             nc.sync.dma_start(out=half[:], in_=w1_rows[:, 2 * u : 2 * u + 2, :])
             w1_raw.append(half)
-        x_rows = xT.rearrange("(p j) t -> p j t", j=PACK)
-        x_raw = []
-        for u in range(2):
-            half = keep.tile([P, 2, T], F32, name=f"x_raw{u}")
-            nc.sync.dma_start(out=half[:], in_=x_rows[:, 2 * u : 2 * u + 2, :])
-            x_raw.append(half)
+        x_raw = keep.tile([P, PACK, T], F32, name="x_raw")
+        nc.sync.dma_start(out=x_raw[:], in_=xT.rearrange("(p j) t -> p j t", j=PACK))
         nc.sync.dma_start(offsets[:], offs)
-        w2_raw = keep.tile([P, PACK, N], F32, name="w2_raw")
-        nc.sync.dma_start(out=w2_raw[:], in_=w2.rearrange("(p j) m -> p j m", j=PACK))
 
         spark = keep.tile([P, 1], F32, name="spark")
         nc.vector.memset(spark[:], 0.0)
@@ -54,84 +46,76 @@ def tile_picked_shuffle_mlp_relu_perm_l_kernel(tc, xT, w1, w2, offs, out):
         w1_g = keep.tile([P, H, PACK], BF16, name="w1_g", align_bytes=64)
         w1_codes = keep.tile([P, H], U32, name="w1_codes", align_bytes=64)
         w1_scales = keep.tile([P, H], U8, name="w1_scales", align_bytes=64)
-        for u in range(2):
-            js = slice(2 * u, 2 * u + 2)
-            nc.vector.tensor_copy(w1_g[:, 0:W1_SPLIT, js], w1_raw[u][:, :, 0:W1_SPLIT].rearrange("p j c -> p c j"))
-            nc.scalar.copy(w1_g[:, W1_SPLIT:H, js], w1_raw[u][:, :, W1_SPLIT:H].rearrange("p j c -> p c j"))
-        nc.vector.quantize_mx(out=w1_codes[:].bitcast(FP8X4), scales=w1_scales[:], in_=w1_g[:].rearrange("p c j -> p (c j)"))
-
         x_g = keep.tile([P, T, PACK], BF16, name="x_g", align_bytes=64)
         x_codes = keep.tile([P, T], U32, name="x_codes", align_bytes=64)
         x_scales = keep.tile([P, T], U8, name="x_scales", align_bytes=64)
-        for u in range(2):
-            js = slice(2 * u, 2 * u + 2)
-            nc.vector.tensor_copy(x_g[:, 0:X_SPLIT, js], x_raw[u][:, :, 0:X_SPLIT].rearrange("p j t -> p t j"))
-            nc.scalar.copy(x_g[:, X_SPLIT:T, js], x_raw[u][:, :, X_SPLIT:T].rearrange("p j t -> p t j"))
-        for e in range(2):
-            ts = slice(e * P, (e + 1) * P)
-            nc.vector.quantize_mx(out=x_codes[:, ts].bitcast(FP8X4), scales=x_scales[:, ts], in_=x_g[:, ts, :].rearrange("p t j -> p (t j)"))
 
-        h_pairs = keep.tile([P, H, 2], BF16, name="h_pairs")
-        for q in range(4):
-            cs = slice(q * P, (q + 1) * P)
-            prod = psum.tile([P, 2, P], F32, name=f"prod{q}")
-            for e in range(2):
-                ts = slice(e * P, (e + 1) * P)
-                nc.tensor.matmul_mx(out=prod[:, e, :], lhsT=x_codes[:, ts].bitcast(FP8X4), lhsT_scale=x_scales[:, ts], rhs=w1_codes[:, cs].bitcast(FP8X4), rhs_scale=w1_scales[:, cs], start=True, stop=True)
-            if q % 2 == 0:
-                nc.scalar.activation(h_pairs[:, cs, :], prod[:].rearrange("p e c -> p c e"), RELU)
+        def interleave(grouped, raw, js, split):
+            for engine_copy, cols in zip((nc.vector.tensor_copy, nc.scalar.copy, nc.scalar.copy), split):
+                engine_copy(grouped[:, cols[0] : cols[1], js], raw[:, :, cols[0] : cols[1]].rearrange("p j c -> p c j"))
+
+        def quantise(codes, scales, grouped, cols):
+            nc.vector.quantize_mx(out=codes[:, cols].bitcast(FP8X4), scales=scales[:, cols], in_=grouped[:, cols, :].rearrange("p c j -> p (c j)"))
+
+        def block(i, width=P):
+            return slice(i * width, (i + 1) * width)
+
+        interleave(w1_g, w1_raw[0], slice(0, 2), [(0, 344), (344, 512)])
+        interleave(w1_g, w1_raw[1], slice(2, 4), [(0, 256), (256, 512)])
+        w2_raw = keep.tile([P, PACK, N], F32, name="w2_raw", tag="late")
+        nc.sync.dma_start(out=w2_raw[:], in_=w2.rearrange("(p j) m -> p j m", j=PACK))
+        quantise(w1_codes, w1_scales, w1_g, block(0, 256))
+        interleave(x_g, x_raw, slice(0, 4), [(0, 96), (96, 128), (128, 256)])
+        quantise(x_codes, x_scales, x_g, block(0))
+        quantise(w1_codes, w1_scales, w1_g, block(1, 256))
+        quantise(x_codes, x_scales, x_g, block(1))
+
+        h0 = keep.tile([P, H], F32, name="h0")
+        h1 = keep.tile([P, H], BF16, name="h1")
+        pieces = [(0, 0, 256), (0, 256, 512), (1, 0, 256), (1, 256, 384), (1, 384, 512)]
+        for i, (e, c0, c1) in enumerate(pieces):
+            prod = psum.tile([P, c1 - c0], F32, name=f"prod{i}")
+            nc.tensor.matmul_mx(out=prod[:], lhsT=x_codes[:, block(e)].bitcast(FP8X4), lhsT_scale=x_scales[:, block(e)], rhs=w1_codes[:, c0:c1].bitcast(FP8X4), rhs_scale=w1_scales[:, c0:c1], start=True, stop=True)
+            if i in (0, 3):
+                nc.vector.tensor_scalar_max((h0, h1)[e][:, c0:c1], prod[:], 0.0)
             else:
-                nc.vector.tensor_scalar_max(h_pairs[:, cs, :], prod[:].rearrange("p e c -> p c e"), 0.0)
+                nc.scalar.activation((h0, h1)[e][:, c0:c1], prod[:], RELU)
+
+        picked = [keep.tile([P, 2, P, 2], BF16, name=f"picked{e}") for e in range(2)]
+        for a in range(2):
+            slots = [picked[e][:, :, 64 * a : 64 * a + 64, :].rearrange("p u m v -> p m u v") for e in range(2)]
+            listed = offsets[:, 16 * a : 16 * a + 16]
+            nc.vector.tensor_copy(slots[0], h0[:].indirect(listed))
+            nc.scalar.activation(slots[1], h1[:].indirect(listed), COPY)
 
         w2_g = keep.tile([P, N, PACK], BF16, name="w2_g", align_bytes=64)
         w2_codes = keep.tile([P, N], U32, name="w2_codes", align_bytes=64)
         w2_scales = keep.tile([P, N], U8, name="w2_scales", align_bytes=64)
-        nc.scalar.copy(w2_g[:], w2_raw[:].rearrange("p j m -> p m j"))
-
-        picked = keep.tile([P, PACK, P, 2], BF16, name="picked")
-        words = picked[:].rearrange("p t m e -> p t (m e)").bitcast(U32)
-        window = h_pairs[:].rearrange("p c e -> p (c e)").bitcast(U32)
-        for a in range(2):
-            nc.vector.tensor_copy(words[:, :, 64 * a : 64 * a + 64].rearrange("p t m -> p m t"), window.indirect(offsets[:, 16 * a : 16 * a + 16]))
-
-        nc.vector.quantize_mx(out=w2_codes[:].bitcast(FP8X4), scales=w2_scales[:], in_=w2_g[:].rearrange("p m j -> p (m j)"))
+        nc.vector.tensor_copy(w2_g[:], w2_raw[:].rearrange("p j m -> p m j"))
+        quantise(w2_codes, w2_scales, w2_g, block(0, N))
 
         hq_g = keep.tile([P, T, PACK], BF16, name="hq_g", align_bytes=64)
         h_codes = keep.tile([P, T], U32, name="h_codes", align_bytes=64)
         h_scales = keep.tile([P, T], U8, name="h_scales", align_bytes=64)
-        picked_words = picked[:].rearrange("p t m e -> p t (m e)").bitcast(F32)
-        turned = []
-        for u in range(2):
-            pair = psum.tile([P, 2, P], F32, name=f"turned{u}")
-            for t in range(2):
-                nc.tensor.transpose(pair[:, t, :], picked_words[:, 2 * u + t, :], ident[:])
-            turned.append(pair[:].bitcast(BF16).rearrange("p t (n e) -> p e n t", e=2))
         for e in range(2):
-            ts = slice(e * P, (e + 1) * P)
-            nc.vector.tensor_copy(hq_g[:, ts, 0:2], turned[0][:, e, :, :])
-            nc.scalar.copy(hq_g[:, ts, 2:4], turned[1][:, e, :, :])
+            turned = psum.tile([P, 2, P], F32, name=f"turned{e}")
+            for u in range(2):
+                nc.tensor.transpose(turned[:, u, :], picked[e][:, u, :, :].rearrange("p m v -> p (m v)").bitcast(F32), ident[:])
+            words = hq_g[:, block(e), :].rearrange("p n t -> p (n t)").bitcast(F32).rearrange("p (n u) -> p n u", u=2)
+            if e == 0:
+                nc.scalar.copy(words, turned[:].rearrange("p u n -> p n u"))
+            else:
+                nc.vector.tensor_copy(words, turned[:].rearrange("p u n -> p n u"))
         out_rows = out.rearrange("(b m) t -> m b t", b=2)
         for e in range(2):
-            ts = slice(e * P, (e + 1) * P)
-            nc.vector.quantize_mx(out=h_codes[:, ts].bitcast(FP8X4), scales=h_scales[:, ts], in_=hq_g[:, ts, :].rearrange("p t j -> p (t j)"))
-            results = []
+            ts = block(e)
+            quantise(h_codes, h_scales, hq_g, ts)
+            res = [psum.tile([P, P], F32, name=f"res{e}{b}", tag=f"prod{2 * e + b}") for b in range(2)]
             for b in range(2):
-                ms = slice(b * P, (b + 1) * P)
-                if e == 0 and b == 1:
-                    res = results[0]
-                elif e == 0:
-                    res = psum.tile([P, 2, P], F32, name="res0")
-                else:
-                    res = psum.tile([P, 2, P], F32, name=f"res1{b}", tag=["res1", "prod0"][b])
-                results.append(res)
-                nc.tensor.matmul_mx(out=res[:, b, :], lhsT=w2_codes[:, ms].bitcast(FP8X4), lhsT_scale=w2_scales[:, ms], rhs=h_codes[:, ts].bitcast(FP8X4), rhs_scale=h_scales[:, ts], start=True, stop=True)
-            if e == 0:
-                o0 = keep.tile([P, 2, P], F32, name="o0")
-                nc.scalar.copy(o0[:], results[0][:])
-                nc.sync.dma_start(out=out_rows[:, :, ts], in_=o0[:])
-            else:
-                o1 = [keep.tile([P, P], F32, name=f"o1{b}") for b in range(2)]
-                nc.scalar.copy(o1[0][:], results[0][:, 0, :])
-                nc.vector.tensor_copy(o1[1][:], results[1][:, 1, :])
-                nc.scalar.dma_start(out=out_rows[:, 0, ts], in_=o1[0][:])
-                nc.sync.dma_start(out=out_rows[:, 1, ts], in_=o1[1][:])
+                ms = block(b)
+                nc.tensor.matmul_mx(out=res[b][:], lhsT=w2_codes[:, ms].bitcast(FP8X4), lhsT_scale=w2_scales[:, ms], rhs=h_codes[:, ts].bitcast(FP8X4), rhs_scale=h_scales[:, ts], start=True, stop=True)
+            done = [keep.tile([P, P], F32, name=f"done{e}{b}") for b in range(2)]
+            nc.scalar.copy(done[0][:], res[0][:])
+            nc.vector.tensor_copy(done[1][:], res[1][:])
+            nc.scalar.dma_start(out=out_rows[:, 0, ts], in_=done[0][:])
+            nc.sync.dma_start(out=out_rows[:, 1, ts], in_=done[1][:])

from contextlib import ExitStack

import concourse.mybir as mybir
from concourse.masks import make_identity

K, T, H, N = 512, 256, 512, 256
P = 128
PACK = 4
FLOPS = 2 * K * H * T + 2 * H * N * T

F32 = mybir.dt.float32
BF16 = mybir.dt.bfloat16
U32 = mybir.dt.uint32
U16 = mybir.dt.uint16
U8 = mybir.dt.uint8
FP8X4 = mybir.dt.float8_e4m3fn_x4
RELU = mybir.ActivationFunctionType.Relu
COPY = mybir.ActivationFunctionType.Copy


def tile_picked_shuffle_mlp_relu_perm_l_kernel(tc, xT, w1, w2, offs, out):
    nc = tc.nc
    with ExitStack() as ctx:
        keep = ctx.enter_context(tc.tile_pool(name="keep", bufs=1))
        psum = ctx.enter_context(tc.psum_pool(name="psum", bufs=1))

        offsets = keep.tile([P, H // 16], U16, name="offsets")

        w1_rows = w1.rearrange("(p j) c -> p j c", j=PACK)
        w1_raw = []
        for u in range(2):
            half = keep.tile([P, 2, H], F32, name=f"w1_raw{u}", tag=["early", "late"][u])
            nc.sync.dma_start(out=half[:], in_=w1_rows[:, 2 * u : 2 * u + 2, :])
            w1_raw.append(half)
        x_raw = keep.tile([P, PACK, T], F32, name="x_raw")
        nc.sync.dma_start(out=x_raw[:], in_=xT.rearrange("(p j) t -> p j t", j=PACK))
        nc.sync.dma_start(offsets[:], offs)

        spark = keep.tile([P, 1], F32, name="spark")
        nc.vector.memset(spark[:], 0.0)
        spark_out = keep.tile([P, 1], F32, name="spark_out")
        nc.scalar.activation(spark_out[:], spark[:], RELU)
        ident = keep.tile([P, P], F32, name="ident")
        make_identity(nc, ident[:])

        w1_g = keep.tile([P, H, PACK], BF16, name="w1_g", align_bytes=64)
        w1_codes = keep.tile([P, H], U32, name="w1_codes", align_bytes=64)
        w1_scales = keep.tile([P, H], U8, name="w1_scales", align_bytes=64)
        x_g = keep.tile([P, T, PACK], BF16, name="x_g", align_bytes=64)
        x_codes = keep.tile([P, T], U32, name="x_codes", align_bytes=64)
        x_scales = keep.tile([P, T], U8, name="x_scales", align_bytes=64)

        def interleave(grouped, raw, js, split):
            for engine_copy, cols in zip((nc.vector.tensor_copy, nc.scalar.copy, nc.scalar.copy), split):
                engine_copy(grouped[:, cols[0] : cols[1], js], raw[:, :, cols[0] : cols[1]].rearrange("p j c -> p c j"))

        def quantise(codes, scales, grouped, cols):
            nc.vector.quantize_mx(out=codes[:, cols].bitcast(FP8X4), scales=scales[:, cols], in_=grouped[:, cols, :].rearrange("p c j -> p (c j)"))

        def block(i, width=P):
            return slice(i * width, (i + 1) * width)

        interleave(w1_g, w1_raw[0], slice(0, 2), [(0, 344), (344, 512)])
        interleave(w1_g, w1_raw[1], slice(2, 4), [(0, 256), (256, 512)])
        w2_raw = keep.tile([P, PACK, N], F32, name="w2_raw", tag="late")
        nc.sync.dma_start(out=w2_raw[:], in_=w2.rearrange("(p j) m -> p j m", j=PACK))
        quantise(w1_codes, w1_scales, w1_g, block(0, 256))
        interleave(x_g, x_raw, slice(0, 4), [(0, 96), (96, 128), (128, 256)])
        quantise(x_codes, x_scales, x_g, block(0))
        quantise(w1_codes, w1_scales, w1_g, block(1, 256))
        quantise(x_codes, x_scales, x_g, block(1))

        h0 = keep.tile([P, H], F32, name="h0")
        h1 = keep.tile([P, H], BF16, name="h1")
        pieces = [(0, 0, 256), (0, 256, 512), (1, 0, 256), (1, 256, 384), (1, 384, 512)]
        for i, (e, c0, c1) in enumerate(pieces):
            prod = psum.tile([P, c1 - c0], F32, name=f"prod{i}")
            nc.tensor.matmul_mx(out=prod[:], lhsT=x_codes[:, block(e)].bitcast(FP8X4), lhsT_scale=x_scales[:, block(e)], rhs=w1_codes[:, c0:c1].bitcast(FP8X4), rhs_scale=w1_scales[:, c0:c1], start=True, stop=True)
            if i in (0, 3):
                nc.vector.tensor_scalar_max((h0, h1)[e][:, c0:c1], prod[:], 0.0)
            else:
                nc.scalar.activation((h0, h1)[e][:, c0:c1], prod[:], RELU)

        picked = [keep.tile([P, 2, P, 2], BF16, name=f"picked{e}") for e in range(2)]
        for a in range(2):
            slots = [picked[e][:, :, 64 * a : 64 * a + 64, :].rearrange("p u m v -> p m u v") for e in range(2)]
            listed = offsets[:, 16 * a : 16 * a + 16]
            nc.vector.tensor_copy(slots[0], h0[:].indirect(listed))
            nc.scalar.activation(slots[1], h1[:].indirect(listed), COPY)

        w2_g = keep.tile([P, N, PACK], BF16, name="w2_g", align_bytes=64)
        w2_codes = keep.tile([P, N], U32, name="w2_codes", align_bytes=64)
        w2_scales = keep.tile([P, N], U8, name="w2_scales", align_bytes=64)
        nc.vector.tensor_copy(w2_g[:], w2_raw[:].rearrange("p j m -> p m j"))
        quantise(w2_codes, w2_scales, w2_g, block(0, N))

        hq_g = keep.tile([P, T, PACK], BF16, name="hq_g", align_bytes=64)
        h_codes = keep.tile([P, T], U32, name="h_codes", align_bytes=64)
        h_scales = keep.tile([P, T], U8, name="h_scales", align_bytes=64)
        for e in range(2):
            turned = psum.tile([P, 2, P], F32, name=f"turned{e}")
            for u in range(2):
                nc.tensor.transpose(turned[:, u, :], picked[e][:, u, :, :].rearrange("p m v -> p (m v)").bitcast(F32), ident[:])
            words = hq_g[:, block(e), :].rearrange("p n t -> p (n t)").bitcast(F32).rearrange("p (n u) -> p n u", u=2)
            if e == 0:
                nc.scalar.copy(words, turned[:].rearrange("p u n -> p n u"))
            else:
                nc.vector.tensor_copy(words, turned[:].rearrange("p u n -> p n u"))
        out_rows = out.rearrange("(b m) t -> m b t", b=2)
        for e in range(2):
            ts = block(e)
            quantise(h_codes, h_scales, hq_g, ts)
            res = [psum.tile([P, P], F32, name=f"res{e}{b}", tag=f"prod{2 * e + b}") for b in range(2)]
            for b in range(2):
                ms = block(b)
                nc.tensor.matmul_mx(out=res[b][:], lhsT=w2_codes[:, ms].bitcast(FP8X4), lhsT_scale=w2_scales[:, ms], rhs=h_codes[:, ts].bitcast(FP8X4), rhs_scale=h_scales[:, ts], start=True, stop=True)
            done = [keep.tile([P, P], F32, name=f"done{e}{b}") for b in range(2)]
            nc.scalar.copy(done[0][:], res[0][:])
            nc.vector.tensor_copy(done[1][:], res[1][:])
            nc.scalar.dma_start(out=out_rows[:, 0, ts], in_=done[0][:])
            nc.sync.dma_start(out=out_rows[:, 1, ts], in_=done[1][:])
